import numpy as np, ml_dtypes
CORES = [24,40,56,80,88,96]
N = 6
TK = 64
COEF = [[3,-2,-1,1,2,2],[-1,1,3,3,1,2],[3,3,2,3,1,2],[-1,-2,-2,1,2,3],[1,1,1,-2,3,-2],[-1,3,-1,3,-1,-2]]
def setup_inputs(rng):
    return {"x": rng.standard_normal((N, 128, TK), dtype=np.float32).astype(ml_dtypes.bfloat16), "a": (rng.standard_normal((N, 128, 128), dtype=np.float32) / 11).astype(ml_dtypes.bfloat16)}
def setup_inputs_big(rng):
    d = setup_inputs(rng)
    for k in ("x", "a"): d[k] = (d[k].astype(np.float32) * 1024.0).astype(d[k].dtype)
    return d
def setup_inputs_small(rng):
    d = setup_inputs(rng)
    for k in ("x", "a"): d[k] = (d[k].astype(np.float32) * (1 / 1024.0)).astype(d[k].dtype)
    return d
def setup_inputs_apart(rng):
    d = setup_inputs(rng)
    f = (10.0 ** rng.permutation(np.linspace(-1.5, 1.5, N))).astype(np.float32).reshape(N, 1, 1)
    for k in ("x", "a"): d[k] = (d[k].astype(np.float32) * f).astype(d[k].dtype)
    return d
def reference(x, a):
    X, A = x.astype(np.float64), a.astype(np.float64)
    y = np.stack([A[r].T @ sum(COEF[r][j] * X[j] for j in range(N)) for r in range(N)])
    return {"y": y.astype(ml_dtypes.bfloat16)}

from concourse.bass import DstId, RemoteDMATransfer
from concourse.mybir import AluOpType

N = 6
TK = 64
K_HAND = 4
K_RELAY = 4
K_PLANE = 8

SCRATCH = {
    "xd": ("dram", [128, TK], "bfloat16"),
    "hd": ("dram", [128, TK], "bfloat16"),
    "xs": ("sbuf", [128, N * TK], "bfloat16"),
    "a1": ("sbuf", [128, 128], "bfloat16"),
    "kc": ("sbuf", [128, 4 * 128], "bfloat16"),
    "sc": ("sbuf", [128, 4 * 128], "bfloat16"),
    "acc": ("psum", [128, TK], "float32"),
    "ys": ("sbuf", [128, TK], "bfloat16"),
}
SEMAPHORES = ["ld", "la", "fill", "scaled", "hin", "sent", "mm", "cp", "st"] + ["arr%d" % j for j in range(N)]


def _engines(avail, k):
    bits = [b for b in range(avail.bit_length()) if (avail >> b) & 1]
    m = 0
    for b in bits[::len(bits) // k][:k]:
        m |= 1 << b
    return m


def _common(topo, src, dsts):
    m = topo.mask(src, dsts[0])
    for d in dsts[1:]:
        m &= topo.mask(src, d)
    return m


def _ids(topo, dsts):
    out = []
    for d in dsts:
        rid, pid, _ = topo.addr(d)
        out.append(DstId(rid=rid, pnc=pid))
    return out


def _plan(cores, topo):
    every = range(topo.CHIPS * topo.CORES_PER_CHIP)
    straight, relay = {}, {}
    for j, s in enumerate(cores):
        straight[j] = [d for d in cores if d != s and topo.may_write(s, d)]
        far = [d for d in cores if d != s and not topo.may_write(s, d)]
        if not far:
            continue
        near = [h for h in every if topo.chip(h) == topo.chip(s) and h not in cores
                and all(topo.may_write(h, d) for d in far)]
        dies = sorted({topo.die(h) for h in near}, key=lambda z: z != topo.die(s))
        pools = [[h for h in near if topo.die(h) == z] for z in dies]
        p = [c for c in cores if c == s or topo.may_write(s, c)].index(s)
        for q, d in enumerate(far):
            pool = pools[(p + q) % len(pools)]
            h = pool[(q // len(pools)) % len(pool)]
            relay.setdefault(h, (j, []))[1].append(d)
    return straight, relay


def _k_plane(n):
    return K_PLANE if n > 1 else K_HAND


def rank_program(g, core, T, topo):
    cores = list(T.cores)
    straight, relay = _plan(cores, topo)

    if core in relay:
        j, dsts = relay[core]
        g.wait_ge(T.sem.hin, K_HAND)
        g.remote_dma_fused([RemoteDMATransfer(
            dst_ids=_ids(topo, dsts), dma_engine_mask=_engines(_common(topo, core, dsts), K_RELAY),
            remote_sem=T.sem["arr%d" % j], srcs=[T.hd[:, :]],
            dsts=[T.xs[:, j * TK:(j + 1) * TK] for _ in dsts], alu_op=0)], local_sem=T.sem.sent)
        g.wait_ge(T.sem.sent, K_RELAY)
        return

    r = T.rank_of(core)
    if r is None:
        return
    coef = T.tables["COEF"][r]
    slot = [T.xs[:, j * TK:(j + 1) * TK] for j in range(N)]

    g.sync.dma_start(T.xd[:, :], T.x[:, :]).then_inc(T.sem.ld, 16)
    g.sync.dma_start(T.a1[:, :], T.a[:, :]).then_inc(T.sem.la, 16)
    g.sync.dma_start(slot[r], T.x[:, :]).then_inc(T.sem["arr%d" % r], 16)

    mine = [h for h in relay if relay[h][0] == r]
    avail = _common(topo, core, mine + straight[r])
    sent = 0
    g.wait_ge(T.sem.ld, 16)
    if mine:
        g.remote_dma_fused([RemoteDMATransfer(
            dst_ids=_ids(topo, mine), dma_engine_mask=_engines(avail, K_HAND), remote_sem=T.sem.hin,
            srcs=[T.xd[:, :]], dsts=[T.hd[:, :] for _ in mine], alu_op=0)], local_sem=T.sem.sent)
        sent += K_HAND
    if straight[r]:
        k = _k_plane(len(straight[r]))
        g.remote_dma_fused([RemoteDMATransfer(
            dst_ids=_ids(topo, straight[r]), dma_engine_mask=_engines(avail, k), remote_sem=T.sem["arr%d" % r],
            srcs=[T.xd[:, :]], dsts=[slot[r] for _ in straight[r]], alu_op=0)], local_sem=T.sem.sent)
        sent += k
    g.wait_ge(T.sem.sent, sent)

    ws = sorted({c for c in coef if c != 1})
    lhs = {1: T.a1[:, :]}
    for i, c in enumerate(ws):
        g.vector.memset(T.kc[:, i * 128:(i + 1) * 128], float(c)).then_inc(T.sem.fill, 1)
        lhs[c] = T.sc[:, i * 128:(i + 1) * 128]
    g.vector.wait_ge(T.sem.fill, len(ws))
    g.vector.wait_ge(T.sem.la, 16)
    for i, c in enumerate(ws):
        g.vector.tensor_tensor(lhs[c], T.a1[:, :], T.kc[:, i * 128:(i + 1) * 128],
                               AluOpType.mult).then_inc(T.sem.scaled, 1)

    incs = {r: 16}
    for j in range(N):
        if core in straight[j]:
            incs[j] = _k_plane(len(straight[j]))
    order = [r] + [j for j in range(N) if j != r and j in incs] + [j for j in range(N) if j not in incs]
    g.tensor.wait_ge(T.sem.la, 16)
    g.tensor.wait_ge(T.sem.scaled, len(ws))
    for i, j in enumerate(order):
        g.tensor.wait_ge(T.sem["arr%d" % j], incs.get(j, K_RELAY))
        mm = g.tensor.matmul(T.acc[:, :], lhs[coef[j]], slot[j], i == 0, i == N - 1)
    mm.then_inc(T.sem.mm, 1)

    g.vector.wait_ge(T.sem.mm, 1)
    g.vector.tensor_copy(T.ys[:, :], T.acc[:, :]).then_inc(T.sem.cp, 1)
    g.scalar.wait_ge(T.sem.cp, 1)
    g.scalar.dma_start(T.y[:, :], T.ys[:, :]).then_inc(T.sem.st, 16)
    g.scalar.wait_ge(T.sem.st, 16)
